import numpy as np
import ml_dtypes


def mxq(x, axis, fmt="e4m3"):
    dtype, down = {"e4m3": (ml_dtypes.float8_e4m3fn, 7), "e5m2": (ml_dtypes.float8_e5m2, 14)}[fmt]
    v = np.moveaxis(np.asarray(x, np.float32).astype(ml_dtypes.bfloat16).astype(np.float64), axis, -1)
    blocks = v.reshape(v.shape[:-1] + (-1, 32))
    amax = np.abs(blocks).max(-1, keepdims=True)
    byte = np.maximum(np.where(amax > 0, np.frexp(amax)[1] - 1 + 127, 0) - down, 1)
    scale = np.exp2(byte - 127.0)
    codes = (blocks / scale).astype(np.float32).astype(dtype).astype(np.float64)
    return np.moveaxis((codes * scale).reshape(v.shape), -1, axis)


WIDE = False


def mx_kscale(k):
    if not WIDE:
        return np.ones(k)
    levels = np.array([10, -10, 5, -5, 0])
    if k % 512:
        return np.exp2(np.random.permutation(np.resize(levels, k // 32))).repeat(32)
    a = np.empty((k // 512, 16))
    for p in range(k // 512):
        a[p, :8] = np.random.permutation(np.resize(levels, 8))
        for g in range(8):
            far = levels[np.abs(levels - a[p, g]) >= 10]
            a[p, g + 8] = far[np.random.randint(len(far))]
    return np.exp2(a.ravel()).repeat(32)


def f64(x):
    return np.asarray(x).astype(np.float64)


def striped(idx):
    return np.tile(idx.reshape(-1, 16).T, (8, 1)).astype(np.uint16)


def unstriped(offs):
    return offs[:16].T.reshape(-1).astype(np.int64)


def pack_weight(w):
    k, n = w.shape
    w = f64(np.asarray(w, np.float32).astype(ml_dtypes.bfloat16)).reshape(k // 32, 32, n)
    amax = np.abs(w).max(1)
    byte = np.clip(np.where(amax > 0, np.frexp(amax)[1] - 1 + 127 - 7, 1), 1, 254)
    scaled = (w * np.exp2(127.0 - byte)[:, None, :]).reshape(k, n).astype(np.float32)
    words = np.ascontiguousarray(scaled.reshape(k // 512, 128, 4, n).transpose(0, 1, 3, 2)).astype(ml_dtypes.float8_e4m3fn).view(np.uint8)
    return words, np.ascontiguousarray(byte.astype(np.uint8).reshape(k // 512, 16, n))


def unpack_weight(words, scales):
    g, p, n, _ = words.shape
    vals = np.ascontiguousarray(words).view(ml_dtypes.float8_e4m3fn).astype(np.float64) * np.repeat(np.exp2(scales.astype(np.float64) - 127.0), 8, axis=1)[..., None]
    return vals.transpose(0, 1, 3, 2).reshape(g * 512, n)


K, T, S, V, H, N = 512, 4096, 1536, 512, 512, 256


def setup_inputs():
    n = np.random.standard_normal
    s = mx_kscale(K)[:, None]
    u = mx_kscale(H)
    packed_xT = pack_weight(n((K, T)) * s)
    packed_w4 = pack_weight(n((H, N)) / np.sqrt(H) / u[:, None])
    return {
        "x_words": packed_xT[0],
        "x_scales": packed_xT[1],
        "w1": (n((K, H)) / np.sqrt(K) / s * u).astype(np.float32),
        "w2": (n((K, H)) / np.sqrt(K) / s).astype(np.float32),
        "w3": (n((K, H)) / np.sqrt(K) / s).astype(np.float32),
        "w4_words": packed_w4[0],
        "w4_scales": packed_w4[1],
        "offs": striped(np.random.permutation(T)[:S]),
    }


def reference(x_words, x_scales, w1, w2, w3, w4_words, w4_scales, offs):
    xq = unpack_weight(x_words, x_scales)[:, unstriped(offs)]
    z = (((mxq(f64(w1), 0, "e4m3").T @ xq[:, :V])) * ((mxq(f64(w2), 0, "e4m3").T @ xq[:, V:2 * V]))) * ((mxq(f64(w3), 0, "e4m3").T @ xq[:, 2 * V:3 * V]))
    return unpack_weight(w4_words, w4_scales).T @ mxq(z, 0, "e4m3")

@@ -1,0 +1,168 @@
+from contextlib import ExitStack
+
+import concourse.mybir as mybir
+
+K, T, V, H, N = 512, 4096, 512, 512, 256
+PIECES = 3
+FLOPS = 2 * K * H * V * PIECES + 2 * H * N * V
+
+F32 = mybir.dt.float32
+BF16 = mybir.dt.bfloat16
+I32 = mybir.dt.int32
+U32 = mybir.dt.uint32
+U16 = mybir.dt.uint16
+U8 = mybir.dt.uint8
+FP8X4 = mybir.dt.float8_e4m3fn_x4
+MULT = mybir.AluOpType.mult
+
+P = 128
+PACK = 4
+CHUNK = 128
+CHUNKS = V // CHUNK
+LIST_COLS = V // 16
+HALF = 2 * P
+
+
+def load_scale_rows(nc, plane, rows):
+    by_row = rows.rearrange("(q r) c -> r q c", r=4)
+    for r in range(4):
+        nc.sync.dma_start(out=plane[r:P:32, :].bitcast(I32), in_=by_row[r].bitcast(I32))
+
+
+def tile_picked_trilin_none_p_kernel(
+    tc, x_words, x_scales, w1, w2, w3, w4_words, w4_scales, offs, out
+):
+    nc = tc.nc
+    with ExitStack() as ctx:
+        keep = ctx.enter_context(tc.tile_pool(name="keep", bufs=1))
+        psum = ctx.enter_context(tc.psum_pool(name="psum", bufs=1))
+
+        offsets = keep.tile([P, PIECES * LIST_COLS], U16, name="offsets")
+        nc.sync.dma_start(offsets[:], offs)
+
+        store_scales = keep.tile([P, T], U8, name="store_scales")
+        nc.vector.memset(store_scales[:, 0 : 3 * T // 4].bitcast(I32), 0)
+        nc.gpsimd.memset(store_scales[:, 3 * T // 4 : T].bitcast(I32), 0)
+        load_scale_rows(nc, store_scales, x_scales[0])
+        store_words = keep.tile([P, T], U32, name="store_words")
+        x_rows = x_words[0].rearrange("p c r -> p (c r)").bitcast(I32)
+        for cols in (slice(0, 512), slice(512, T)):
+            nc.sync.dma_start(out=store_words[:, cols].bitcast(I32), in_=x_rows[:, cols])
+        raw = []
+        for d, w in enumerate((w1, w2, w3)):
+            rows = keep.tile([P, PACK, H], F32, name=f"raw{d}")
+            nc.sync.dma_start(out=rows[:], in_=w.rearrange("(p j) h -> p j h", j=PACK))
+            raw.append(rows)
+        last_codes = keep.tile([P, N], U32, name="last_codes", align_bytes=64)
+        nc.sync.dma_start(
+            out=last_codes[:].bitcast(I32),
+            in_=w4_words[0].rearrange("p c r -> p (c r)").bitcast(I32),
+        )
+        last_scales = keep.tile([P, N], U8, name="last_scales", align_bytes=64)
+        nc.gpsimd.memset(last_scales[:].bitcast(I32), 0)
+        load_scale_rows(nc, last_scales, w4_scales[0])
+
+        picked_scales = keep.tile([P, PIECES * V], U8, name="picked_scales", align_bytes=64)
+        nc.vector.tensor_copy(picked_scales[:], store_scales[:].indirect(offsets[:]))
+        picked_words = []
+
+        def pick_words(d, tag):
+            words = keep.tile([P, V], U32, name=f"picked_words{d}", tag=tag, align_bytes=64)
+            piece = offsets[:, d * LIST_COLS : (d + 1) * LIST_COLS]
+            nc.vector.tensor_copy(words[:], store_words[:].indirect(piece))
+            picked_words.append(words)
+
+        pick_words(0, "picked0")
+        pick_words(1, "picked1")
+
+        def quantize_weights(d):
+            halves = []
+            for u in range(2):
+                rounded = keep.tile([P, PACK * HALF], BF16, name=f"rounded{d}_{u}", tag=f"rounded{d}_{u}", align_bytes=64)
+                src = raw[d][:].rearrange("p (a b) (m t) -> p m a t b", b=2, t=PACK)[:, :, :, 2 * u : 2 * u + 2, :]
+                dst = rounded[:].rearrange("p (t m a b) -> p m a t b", t=2, a=2, b=2)
+                if u == 0:
+                    nc.scalar.copy(out=dst, in_=src)
+                else:
+                    nc.vector.tensor_copy(out=dst, in_=src)
+                halves.append(rounded)
+            planes = {}
+            for u in (1, 0):
+                codes = keep.tile([P, HALF], U32, name=f"w_codes{d}_{u}", align_bytes=64)
+                scales = keep.tile([P, HALF], U8, name=f"w_scales{d}_{u}", align_bytes=64)
+                nc.vector.quantize_mx(out=codes[:].bitcast(FP8X4), scales=scales[:], in_=halves[u][:])
+                planes[u] = (codes, scales)
+            return planes
+
+        def first_product(d, planes, c, bank):
+            acc = psum.tile([P, PACK, CHUNK], F32, name=f"acc{d}_{c}", tag=f"bank{bank}")
+            cols = slice(c * CHUNK, (c + 1) * CHUNK)
+            scale_cols = slice(d * V + c * CHUNK, d * V + (c + 1) * CHUNK)
+            for t in (2, 3, 0, 1):
+                codes, scales = planes[t // 2]
+                w_cols = slice((t % 2) * P, (t % 2 + 1) * P)
+                nc.tensor.matmul_mx(
+                    out=acc[:, t, :],
+                    lhsT=codes[:, w_cols].bitcast(FP8X4),
+                    lhsT_scale=scales[:, w_cols],
+                    rhs=picked_words[d][:, cols].bitcast(FP8X4),
+                    rhs_scale=picked_scales[:, scale_cols],
+                    start=True,
+                    stop=True,
+                )
+            return acc[:].rearrange("p t v -> p v t")
+
+        def woven(tile):
+            return tile[:].rearrange("p (v t) -> p v t", t=PACK)
+
+        planes = quantize_weights(0)
+        pick_words(2, "rounded0_0")
+        first_acc = [first_product(0, planes, c, c) for c in range(CHUNKS)]
+        planes = quantize_weights(1)
+        first = []
+        for c in range(CHUNKS):
+            held = keep.tile([P, CHUNK * PACK], F32, name=f"first{c}")
+            nc.scalar.copy(out=woven(held), in_=first_acc[c])
+            first.append(held)
+        second_acc = [first_product(1, planes, c, CHUNKS + c) for c in range(CHUNKS)]
+        pair = []
+        for c in range(CHUNKS):
+            both = keep.tile([P, CHUNK * PACK], F32, name=f"pair{c}")
+            nc.vector.tensor_tensor(out=woven(both), in0=second_acc[c], in1=woven(first[c]), op=MULT)
+            pair.append(both)
+        planes = quantize_weights(2)
+
+        def third(c):
+            acc = first_product(2, planes, c, c)
+            z = keep.tile([P, CHUNK * PACK], BF16, name=f"z{c}", align_bytes=64)
+            nc.vector.tensor_tensor(out=woven(z), in0=acc, in1=woven(pair[c]), op=MULT)
+            return z
+
+        def finish(c, z):
+            codes = keep.tile([P, CHUNK], U32, name=f"z_codes{c}", align_bytes=64)
+            scales = keep.tile([P, CHUNK], U8, name=f"z_scales{c}", align_bytes=64)
+            nc.vector.quantize_mx(out=codes[:].bitcast(FP8X4), scales=scales[:], in_=z[:])
+            acc = psum.tile([P, N // P, CHUNK], F32, name=f"out_acc{c}", tag=f"bank{CHUNKS + c}")
+            for a in range(N // P):
+                m_cols = slice(a * P, (a + 1) * P)
+                nc.tensor.matmul_mx(
+                    out=acc[:, a, :],
+                    lhsT=last_codes[:, m_cols].bitcast(FP8X4),
+                    lhsT_scale=last_scales[:, m_cols],
+                    rhs=codes[:].bitcast(FP8X4),
+                    rhs_scale=scales[:],
+                    start=True,
+                    stop=True,
+                )
+            result = keep.tile([P, N // P, CHUNK], F32, name=f"result{c}")
+            nc.scalar.copy(out=result[:], in_=acc[:])
+            nc.sync.dma_start(
+                out=out.rearrange("(a p) v -> p a v", p=P)[:, :, c * CHUNK : (c + 1) * CHUNK],
+                in_=result[:],
+            )
+
+        zs = [third(0)]
+        for c in range(1, CHUNKS):
+            zs.append(third(c))
+            finish(c - 1, zs[c - 1])
+        finish(CHUNKS - 1, zs[CHUNKS - 1])

@@ -50,7 +50,7 @@ def tile_picked_trilin_none_p_kernel(
             nc.sync.dma_start(out=store_words[:, cols].bitcast(I32), in_=x_rows[:, cols])
         raw = []
         for d, w in enumerate((w1, w2, w3)):
-            rows = keep.tile([P, PACK, H], F32, name=f"raw{d}")
+            rows = keep.tile([P, PACK, H], F32, name=f"raw{d}", tag=f"raw{d}")
             nc.sync.dma_start(out=rows[:], in_=w.rearrange("(p j) h -> p j h", j=PACK))
             raw.append(rows)
         last_codes = keep.tile([P, N], U32, name="last_codes", align_bytes=64)
@@ -74,31 +74,31 @@ def tile_picked_trilin_none_p_kernel(
 
         pick_words(0, "picked0")
         pick_words(1, "picked1")
+        pick_words(2, "picked2")
+
+        def round_half(d, u, copy):
+            rounded = keep.tile([P, PACK * HALF], BF16, name=f"rounded{d}_{u}", tag=f"rounded{d}_{u}", align_bytes=64)
+            src = raw[d][:].rearrange("p (a b) (m t) -> p m a t b", b=2, t=PACK)[:, :, :, 2 * u : 2 * u + 2, :]
+            copy(out=rounded[:].rearrange("p (t m a b) -> p m a t b", t=2, a=2, b=2), in_=src)
+            return rounded
+
+        def quantize_half(d, u, rounded):
+            codes = keep.tile([P, HALF], U32, name=f"w_codes{d}_{u}", align_bytes=64)
+            scales = keep.tile([P, HALF], U8, name=f"w_scales{d}_{u}", align_bytes=64)
+            nc.vector.quantize_mx(out=codes[:].bitcast(FP8X4), scales=scales[:], in_=rounded[:])
+            return codes, scales
 
         def quantize_weights(d):
-            halves = []
-            for u in range(2):
-                rounded = keep.tile([P, PACK * HALF], BF16, name=f"rounded{d}_{u}", tag=f"rounded{d}_{u}", align_bytes=64)
-                src = raw[d][:].rearrange("p (a b) (m t) -> p m a t b", b=2, t=PACK)[:, :, :, 2 * u : 2 * u + 2, :]
-                dst = rounded[:].rearrange("p (t m a b) -> p m a t b", t=2, a=2, b=2)
-                if u == 0:
-                    nc.scalar.copy(out=dst, in_=src)
-                else:
-                    nc.vector.tensor_copy(out=dst, in_=src)
-                halves.append(rounded)
-            planes = {}
-            for u in (1, 0):
-                codes = keep.tile([P, HALF], U32, name=f"w_codes{d}_{u}", align_bytes=64)
-                scales = keep.tile([P, HALF], U8, name=f"w_scales{d}_{u}", align_bytes=64)
-                nc.vector.quantize_mx(out=codes[:].bitcast(FP8X4), scales=scales[:], in_=halves[u][:])
-                planes[u] = (codes, scales)
-            return planes
+            low = round_half(d, 0, nc.scalar.copy)
+            high = round_half(d, 1, nc.vector.tensor_copy)
+            high_planes = quantize_half(d, 1, high)
+            return [quantize_half(d, 0, low), high_planes]
 
         def first_product(d, planes, c, bank):
             acc = psum.tile([P, PACK, CHUNK], F32, name=f"acc{d}_{c}", tag=f"bank{bank}")
             cols = slice(c * CHUNK, (c + 1) * CHUNK)
             scale_cols = slice(d * V + c * CHUNK, d * V + (c + 1) * CHUNK)
-            for t in (2, 3, 0, 1):
+            for t in range(PACK):
                 codes, scales = planes[t // 2]
                 w_cols = slice((t % 2) * P, (t % 2 + 1) * P)
                 nc.tensor.matmul_mx(
@@ -113,40 +113,62 @@ def tile_picked_trilin_none_p_kernel(
             return acc[:].rearrange("p t v -> p v t")
 
         def woven(tile):
-            return tile[:].rearrange("p (v t) -> p v t", t=PACK)
+            return tile.rearrange("p (v t) -> p v t", t=PACK)
 
-        planes = quantize_weights(0)
-        pick_words(2, "rounded0_0")
-        first_acc = [first_product(0, planes, c, c) for c in range(CHUNKS)]
-        planes = quantize_weights(1)
-        first = []
+        first_planes = [quantize_half(0, u, round_half(0, u, nc.scalar.copy)) for u in range(2)]
+        second_planes = quantize_weights(1)
+        first_acc, second_acc = [], []
         for c in range(CHUNKS):
-            held = keep.tile([P, CHUNK * PACK], F32, name=f"first{c}")
-            nc.scalar.copy(out=woven(held), in_=first_acc[c])
-            first.append(held)
-        second_acc = [first_product(1, planes, c, CHUNKS + c) for c in range(CHUNKS)]
-        pair = []
-        for c in range(CHUNKS):
+            first_acc.append(first_product(0, first_planes, c, c))
+            second_acc.append(first_product(1, second_planes, c, CHUNKS + c))
+
+        def hold_first(chunks, tag):
+            held = keep.tile([P, len(chunks), CHUNK * PACK], F32, name=f"first{chunks[0]}", tag=tag)
+            for i, c in enumerate(chunks):
+                nc.scalar.copy(out=woven(held[:, i, :]), in_=first_acc[c])
+            return [held[:, i, :] for i in range(len(chunks))]
+
+        def multiply_pair(c):
             both = keep.tile([P, CHUNK * PACK], F32, name=f"pair{c}")
-            nc.vector.tensor_tensor(out=woven(both), in0=second_acc[c], in1=woven(first[c]), op=MULT)
-            pair.append(both)
-        planes = quantize_weights(2)
+            nc.vector.tensor_tensor(out=woven(both[:]), in0=second_acc[c], in1=woven(first[c]), op=MULT)
+            return both
 
-        def third(c):
+        first = hold_first([0, 1], "first_early")
+        low = round_half(2, 0, nc.scalar.copy)
+        high = keep.tile([P, PACK * HALF], BF16, name="rounded2_1", align_bytes=64)
+        nc.gpsimd.tensor_scalar(
+            out=high[:].rearrange("p (t m j) -> p m t j", t=2, j=PACK),
+            in0=raw[2][:].rearrange("p j (m t) -> p m t j", t=PACK)[:, :, 2:4, :],
+            scalar1=1.0,
+            scalar2=0.0,
+            op0=MULT,
+            op1=mybir.AluOpType.add,
+        )
+        first = first + hold_first([2, 3], "raw2")
+        pair = [multiply_pair(0), multiply_pair(1)]
+        planes = [quantize_half(2, 0, low), quantize_half(2, 1, high)]
+        pair.append(multiply_pair(2))
+        second_last = keep.tile([P, CHUNK * PACK], F32, name="second_last")
+        nc.scalar.copy(out=woven(second_last[:]), in_=second_acc[3])
+        both = keep.tile([P, CHUNK * PACK], F32, name="pair3")
+        nc.gpsimd.tensor_tensor(out=both[:], in0=second_last[:], in1=first[3], op=MULT)
+        pair.append(both)
+
+        def third(c, z):
             acc = first_product(2, planes, c, c)
-            z = keep.tile([P, CHUNK * PACK], BF16, name=f"z{c}", align_bytes=64)
-            nc.vector.tensor_tensor(out=woven(z), in0=acc, in1=woven(pair[c]), op=MULT)
-            return z
+            nc.vector.tensor_tensor(out=woven(z), in0=acc, in1=woven(pair[c][:]), op=MULT)
 
-        def finish(c, z):
-            codes = keep.tile([P, CHUNK], U32, name=f"z_codes{c}", align_bytes=64)
-            scales = keep.tile([P, CHUNK], U8, name=f"z_scales{c}", align_bytes=64)
+        def finish(c0, z, banks, copies):
+            width = z.shape[1] // PACK
+            codes = keep.tile([P, width], U32, name=f"z_codes{c0}", align_bytes=64)
+            scales = keep.tile([P, width], U8, name=f"z_scales{c0}", align_bytes=64)
             nc.vector.quantize_mx(out=codes[:].bitcast(FP8X4), scales=scales[:], in_=z[:])
-            acc = psum.tile([P, N // P, CHUNK], F32, name=f"out_acc{c}", tag=f"bank{CHUNKS + c}")
+            result = keep.tile([P, N // P, width], F32, name=f"result{c0}")
             for a in range(N // P):
+                acc = psum.tile([P, width], F32, name=f"out_acc{c0}_{a}", tag=f"bank{banks[a]}")
                 m_cols = slice(a * P, (a + 1) * P)
                 nc.tensor.matmul_mx(
-                    out=acc[:, a, :],
+                    out=acc[:],
                     lhsT=last_codes[:, m_cols].bitcast(FP8X4),
                     lhsT_scale=last_scales[:, m_cols],
                     rhs=codes[:].bitcast(FP8X4),
@@ -154,15 +176,20 @@ def tile_picked_trilin_none_p_kernel(
                     start=True,
                     stop=True,
                 )
-            result = keep.tile([P, N // P, CHUNK], F32, name=f"result{c}")
-            nc.scalar.copy(out=result[:], in_=acc[:])
+                copies[a](out=result[:, a, :], in_=acc[:])
             nc.sync.dma_start(
-                out=out.rearrange("(a p) v -> p a v", p=P)[:, :, c * CHUNK : (c + 1) * CHUNK],
+                out=out.rearrange("(a p) v -> p a v", p=P)[:, :, c0 * CHUNK : c0 * CHUNK + width],
                 in_=result[:],
             )
 
-        zs = [third(0)]
-        for c in range(1, CHUNKS):
-            zs.append(third(c))
-            finish(c - 1, zs[c - 1])
-        finish(CHUNKS - 1, zs[CHUNKS - 1])
+        span = CHUNK * PACK
+        z01 = keep.tile([P, 2 * span], BF16, name="z01", align_bytes=64)
+        z2 = keep.tile([P, span], BF16, name="z2", align_bytes=64)
+        z3 = keep.tile([P, span], BF16, name="z3", align_bytes=64)
+        third(0, z01[:, 0:span])
+        third(1, z01[:, span : 2 * span])
+        third(2, z2[:])
+        finish(0, z01, (4, 5), (nc.scalar.copy, nc.scalar.copy))
+        third(3, z3[:])
+        finish(2, z2, (6, 7), (nc.scalar.copy, nc.scalar.copy))
+        finish(3, z3, (0, 1), (nc.scalar.copy, nc.vector.tensor_copy))

@@ -14,19 +14,33 @@ U16 = mybir.dt.uint16
 U8 = mybir.dt.uint8
 FP8X4 = mybir.dt.float8_e4m3fn_x4
 MULT = mybir.AluOpType.mult
+ADD = mybir.AluOpType.add
 
 P = 128
 PACK = 4
+QUADRANT = 32
 CHUNK = 128
 CHUNKS = V // CHUNK
+SPAN = CHUNK * PACK
 LIST_COLS = V // 16
 HALF = 2 * P
+VECTOR_CLEARS = 3 * T // 4
+FIRST_PART = 768
 
 
 def load_scale_rows(nc, plane, rows):
-    by_row = rows.rearrange("(q r) c -> r q c", r=4)
-    for r in range(4):
-        nc.sync.dma_start(out=plane[r:P:32, :].bitcast(I32), in_=by_row[r].bitcast(I32))
+    by_place = rows.rearrange("(q r) c -> r q c", r=PACK)
+    for r in range(PACK):
+        nc.sync.dma_start(out=plane[r:P:QUADRANT, :].bitcast(I32), in_=by_place[r].bitcast(I32))
+
+
+def woven(values):
+    return values.rearrange("p (v t) -> p v t", t=PACK)
+
+
+def half_views(rows, u, rounded):
+    source = rows.rearrange("p (a b) (m t) -> p m a t b", b=2, t=PACK)[:, :, :, 2 * u : 2 * u + 2, :]
+    return rounded.rearrange("p (t m a b) -> p m a t b", t=2, a=2, b=2), source
 
 
 def tile_picked_trilin_none_p_kernel(
@@ -41,70 +55,64 @@ def tile_picked_trilin_none_p_kernel(
         nc.sync.dma_start(offsets[:], offs)
 
         store_scales = keep.tile([P, T], U8, name="store_scales")
-        nc.vector.memset(store_scales[:, 0 : 3 * T // 4].bitcast(I32), 0)
-        nc.gpsimd.memset(store_scales[:, 3 * T // 4 : T].bitcast(I32), 0)
+        nc.vector.memset(store_scales[:, 0:VECTOR_CLEARS].bitcast(I32), 0)
+        nc.gpsimd.memset(store_scales[:, VECTOR_CLEARS:T].bitcast(I32), 0)
         load_scale_rows(nc, store_scales, x_scales[0])
         store_words = keep.tile([P, T], U32, name="store_words")
         x_rows = x_words[0].rearrange("p c r -> p (c r)").bitcast(I32)
-        for cols in (slice(0, 512), slice(512, T)):
+        for cols in (slice(0, FIRST_PART), slice(FIRST_PART, T)):
             nc.sync.dma_start(out=store_words[:, cols].bitcast(I32), in_=x_rows[:, cols])
         raw = []
         for d, w in enumerate((w1, w2, w3)):
             rows = keep.tile([P, PACK, H], F32, name=f"raw{d}", tag=f"raw{d}")
             nc.sync.dma_start(out=rows[:], in_=w.rearrange("(p j) h -> p j h", j=PACK))
             raw.append(rows)
-        last_codes = keep.tile([P, N], U32, name="last_codes", align_bytes=64)
+        w4_codes = keep.tile([P, N], U32, name="w4_codes", align_bytes=64)
         nc.sync.dma_start(
-            out=last_codes[:].bitcast(I32),
+            out=w4_codes[:].bitcast(I32),
             in_=w4_words[0].rearrange("p c r -> p (c r)").bitcast(I32),
         )
-        last_scales = keep.tile([P, N], U8, name="last_scales", align_bytes=64)
-        nc.gpsimd.memset(last_scales[:].bitcast(I32), 0)
-        load_scale_rows(nc, last_scales, w4_scales[0])
+        w4_plane = keep.tile([P, N], U8, name="w4_plane", align_bytes=64)
+        nc.gpsimd.memset(w4_plane[:].bitcast(I32), 0)
+        load_scale_rows(nc, w4_plane, w4_scales[0])
+
+        warm = keep.tile([P, 2, 8], F32, name="warm")
+        nc.gpsimd.memset(warm[:, 0, :], 0.0)
+        nc.scalar.copy(out=warm[:, 1, :], in_=warm[:, 0, :])
 
         picked_scales = keep.tile([P, PIECES * V], U8, name="picked_scales", align_bytes=64)
         nc.vector.tensor_copy(picked_scales[:], store_scales[:].indirect(offsets[:]))
         picked_words = []
-
-        def pick_words(d, tag):
-            words = keep.tile([P, V], U32, name=f"picked_words{d}", tag=tag, align_bytes=64)
+        for d in range(PIECES):
+            words = keep.tile([P, V], U32, name=f"picked_words{d}", align_bytes=64)
             piece = offsets[:, d * LIST_COLS : (d + 1) * LIST_COLS]
             nc.vector.tensor_copy(words[:], store_words[:].indirect(piece))
             picked_words.append(words)
 
-        pick_words(0, "picked0")
-        pick_words(1, "picked1")
-        pick_words(2, "picked2")
+        def quantize(name, rounded):
+            width = rounded.shape[1] // PACK
+            codes = keep.tile([P, width], U32, name=f"{name}_codes", align_bytes=64)
+            plane = keep.tile([P, width], U8, name=f"{name}_plane", align_bytes=64)
+            nc.vector.quantize_mx(out=codes[:].bitcast(FP8X4), scales=plane[:], in_=rounded)
+            return codes, plane
 
         def round_half(d, u, copy):
-            rounded = keep.tile([P, PACK * HALF], BF16, name=f"rounded{d}_{u}", tag=f"rounded{d}_{u}", align_bytes=64)
-            src = raw[d][:].rearrange("p (a b) (m t) -> p m a t b", b=2, t=PACK)[:, :, :, 2 * u : 2 * u + 2, :]
-            copy(out=rounded[:].rearrange("p (t m a b) -> p m a t b", t=2, a=2, b=2), in_=src)
-            return rounded
+            rounded = keep.tile([P, PACK * HALF], BF16, name=f"rounded{d}_{u}", align_bytes=64)
+            target, source = half_views(raw[d][:], u, rounded[:])
+            copy(out=target, in_=source)
+            return rounded[:]
 
-        def quantize_half(d, u, rounded):
-            codes = keep.tile([P, HALF], U32, name=f"w_codes{d}_{u}", align_bytes=64)
-            scales = keep.tile([P, HALF], U8, name=f"w_scales{d}_{u}", align_bytes=64)
-            nc.vector.quantize_mx(out=codes[:].bitcast(FP8X4), scales=scales[:], in_=rounded[:])
-            return codes, scales
-
-        def quantize_weights(d):
-            low = round_half(d, 0, nc.scalar.copy)
-            high = round_half(d, 1, nc.vector.tensor_copy)
-            high_planes = quantize_half(d, 1, high)
-            return [quantize_half(d, 0, low), high_planes]
-
-        def first_product(d, planes, c, bank):
+        def factor(d, halves, c, bank, tile_order):
             acc = psum.tile([P, PACK, CHUNK], F32, name=f"acc{d}_{c}", tag=f"bank{bank}")
             cols = slice(c * CHUNK, (c + 1) * CHUNK)
             scale_cols = slice(d * V + c * CHUNK, d * V + (c + 1) * CHUNK)
-            for t in range(PACK):
-                codes, scales = planes[t // 2]
+            for t in tile_order:
+                codes, plane = halves[t // 2]
                 w_cols = slice((t % 2) * P, (t % 2 + 1) * P)
                 nc.tensor.matmul_mx(
                     out=acc[:, t, :],
                     lhsT=codes[:, w_cols].bitcast(FP8X4),
-                    lhsT_scale=scales[:, w_cols],
+                    lhsT_scale=plane[:, w_cols],
                     rhs=picked_words[d][:, cols].bitcast(FP8X4),
                     rhs_scale=picked_scales[:, scale_cols],
                     start=True,
@@ -112,84 +120,84 @@ def tile_picked_trilin_none_p_kernel(
                 )
             return acc[:].rearrange("p t v -> p v t")
 
-        def woven(tile):
-            return tile.rearrange("p (v t) -> p v t", t=PACK)
+        w1_halves = [quantize(f"w1_{u}", round_half(0, u, nc.scalar.copy)) for u in range(2)]
+        w2_low = round_half(1, 0, nc.scalar.copy)
+        w2_high = round_half(1, 1, nc.vector.tensor_copy)
+        w2_high_half = quantize("w2_1", w2_high)
+        w2_halves = [quantize("w2_0", w2_low), w2_high_half]
 
-        first_planes = [quantize_half(0, u, round_half(0, u, nc.scalar.copy)) for u in range(2)]
-        second_planes = quantize_weights(1)
         first_acc, second_acc = [], []
         for c in range(CHUNKS):
-            first_acc.append(first_product(0, first_planes, c, c))
-            second_acc.append(first_product(1, second_planes, c, CHUNKS + c))
+            first_acc.append(factor(0, w1_halves, c, c, (0, 1, 2, 3)))
+            second_acc.append(factor(1, w2_halves, c, CHUNKS + c, (2, 3, 0, 1)))
 
         def hold_first(chunks, tag):
-            held = keep.tile([P, len(chunks), CHUNK * PACK], F32, name=f"first{chunks[0]}", tag=tag)
-            for i, c in enumerate(chunks):
-                nc.scalar.copy(out=woven(held[:, i, :]), in_=first_acc[c])
-            return [held[:, i, :] for i in range(len(chunks))]
+            held = keep.tile([P, len(chunks), SPAN], F32, name=f"first{chunks[0]}", tag=tag)
+            for place, c in enumerate(chunks):
+                nc.scalar.copy(out=woven(held[:, place, :]), in_=first_acc[c])
+            return [held[:, place, :] for place in range(len(chunks))]
 
-        def multiply_pair(c):
-            both = keep.tile([P, CHUNK * PACK], F32, name=f"pair{c}")
+        def multiply_pair(c, tag):
+            both = keep.tile([P, SPAN], F32, name=f"pair{c}", tag=tag, align_bytes=64)
             nc.vector.tensor_tensor(out=woven(both[:]), in0=second_acc[c], in1=woven(first[c]), op=MULT)
             return both
 
         first = hold_first([0, 1], "first_early")
-        low = round_half(2, 0, nc.scalar.copy)
-        high = keep.tile([P, PACK * HALF], BF16, name="rounded2_1", align_bytes=64)
+        w3_rounded = keep.tile([P, 2, PACK * HALF], BF16, name="w3_rounded", tag="w3_rounded", align_bytes=64)
+        target, source = half_views(raw[2][:], 0, w3_rounded[:, 0, :])
+        nc.scalar.copy(out=target, in_=source)
         nc.gpsimd.tensor_scalar(
-            out=high[:].rearrange("p (t m j) -> p m t j", t=2, j=PACK),
+            out=w3_rounded[:, 1, :].rearrange("p (t m j) -> p m t j", t=2, j=PACK),
             in0=raw[2][:].rearrange("p j (m t) -> p m t j", t=PACK)[:, :, 2:4, :],
             scalar1=1.0,
             scalar2=0.0,
             op0=MULT,
-            op1=mybir.AluOpType.add,
+            op1=ADD,
         )
         first = first + hold_first([2, 3], "raw2")
-        pair = [multiply_pair(0), multiply_pair(1)]
-        planes = [quantize_half(2, 0, low), quantize_half(2, 1, high)]
-        pair.append(multiply_pair(2))
-        second_last = keep.tile([P, CHUNK * PACK], F32, name="second_last")
-        nc.scalar.copy(out=woven(second_last[:]), in_=second_acc[3])
-        both = keep.tile([P, CHUNK * PACK], F32, name="pair3")
-        nc.gpsimd.tensor_tensor(out=both[:], in0=second_last[:], in1=first[3], op=MULT)
-        pair.append(both)
 
-        def third(c, z):
-            acc = first_product(2, planes, c, c)
+        pair = [multiply_pair(0, "pair0"), multiply_pair(1, "pair1")]
+        w3_codes, w3_plane = quantize("w3", w3_rounded[:].rearrange("p u c -> p (u c)"))
+        w3_halves = [(w3_codes[:, u * HALF : (u + 1) * HALF], w3_plane[:, u * HALF : (u + 1) * HALF]) for u in range(2)]
+        pair.append(multiply_pair(2, "w3_rounded"))
+        second_last = keep.tile([P, SPAN], F32, name="second_last")
+        nc.scalar.copy(out=woven(second_last[:]), in_=second_acc[3])
+        pair_last = keep.tile([P, SPAN], F32, name="pair3")
+        nc.gpsimd.tensor_tensor(out=pair_last[:], in0=second_last[:], in1=first[3], op=MULT)
+        pair.append(pair_last)
+
+        def multiply_third(c, z):
+            acc = factor(2, w3_halves, c, c, (0, 1, 2, 3))
             nc.vector.tensor_tensor(out=woven(z), in0=acc, in1=woven(pair[c][:]), op=MULT)
 
-        def finish(c0, z, banks, copies):
+        def finish(c, z, banks, copies, queues):
+            codes, plane = quantize(f"z{c}", z)
             width = z.shape[1] // PACK
-            codes = keep.tile([P, width], U32, name=f"z_codes{c0}", align_bytes=64)
-            scales = keep.tile([P, width], U8, name=f"z_scales{c0}", align_bytes=64)
-            nc.vector.quantize_mx(out=codes[:].bitcast(FP8X4), scales=scales[:], in_=z[:])
-            result = keep.tile([P, N // P, width], F32, name=f"result{c0}")
-            for a in range(N // P):
-                acc = psum.tile([P, width], F32, name=f"out_acc{c0}_{a}", tag=f"bank{banks[a]}")
-                m_cols = slice(a * P, (a + 1) * P)
+            for block in range(N // P):
+                acc = psum.tile([P, width], F32, name=f"out_acc{c}_{block}", tag=f"bank{banks[block]}")
+                out_rows = slice(block * P, (block + 1) * P)
                 nc.tensor.matmul_mx(
                     out=acc[:],
-                    lhsT=last_codes[:, m_cols].bitcast(FP8X4),
-                    lhsT_scale=last_scales[:, m_cols],
+                    lhsT=w4_codes[:, out_rows].bitcast(FP8X4),
+                    lhsT_scale=w4_plane[:, out_rows],
                     rhs=codes[:].bitcast(FP8X4),
-                    rhs_scale=scales[:],
+                    rhs_scale=plane[:],
                     start=True,
                     stop=True,
                 )
-                copies[a](out=result[:, a, :], in_=acc[:])
-            nc.sync.dma_start(
-                out=out.rearrange("(a p) v -> p a v", p=P)[:, :, c0 * CHUNK : c0 * CHUNK + width],
-                in_=result[:],
-            )
+                result = keep.tile([P, width], F32, name=f"result{c}_{block}")
+                copies[block](out=result[:], in_=acc[:])
+                queues[block].dma_start(out=out[out_rows, c * CHUNK : c * CHUNK + width], in_=result[:])
 
-        span = CHUNK * PACK
-        z01 = keep.tile([P, 2 * span], BF16, name="z01", align_bytes=64)
-        z2 = keep.tile([P, span], BF16, name="z2", align_bytes=64)
-        z3 = keep.tile([P, span], BF16, name="z3", align_bytes=64)
-        third(0, z01[:, 0:span])
-        third(1, z01[:, span : 2 * span])
-        third(2, z2[:])
-        finish(0, z01, (4, 5), (nc.scalar.copy, nc.scalar.copy))
-        third(3, z3[:])
-        finish(2, z2, (6, 7), (nc.scalar.copy, nc.scalar.copy))
-        finish(3, z3, (0, 1), (nc.scalar.copy, nc.vector.tensor_copy))
+        z01 = keep.tile([P, 2 * SPAN], BF16, name="z01", align_bytes=64)
+        z2 = keep.tile([P, SPAN], BF16, name="z2", align_bytes=64)
+        z3 = keep.tile([P, SPAN], BF16, name="z3", align_bytes=64)
+        on_scalar = (nc.scalar.copy, nc.scalar.copy)
+        on_sync = (nc.sync, nc.sync)
+        multiply_third(0, z01[:, 0:SPAN])
+        multiply_third(1, z01[:, SPAN : 2 * SPAN])
+        multiply_third(2, z2[:])
+        finish(0, z01[:], (4, 5), on_scalar, on_sync)
+        multiply_third(3, z3[:])
+        finish(2, z2[:], (6, 7), on_scalar, on_sync)
+        finish(3, z3[:], (0, 1), (nc.scalar.copy, nc.vector.tensor_copy), (nc.scalar, nc.sync))

from contextlib import ExitStack

import concourse.mybir as mybir

K, T, V, H, N = 512, 4096, 512, 512, 256
PIECES = 3
FLOPS = 2 * K * H * V * PIECES + 2 * H * N * V

F32 = mybir.dt.float32
BF16 = mybir.dt.bfloat16
I32 = mybir.dt.int32
U32 = mybir.dt.uint32
U16 = mybir.dt.uint16
U8 = mybir.dt.uint8
FP8X4 = mybir.dt.float8_e4m3fn_x4
MULT = mybir.AluOpType.mult
ADD = mybir.AluOpType.add

P = 128
PACK = 4
QUADRANT = 32
CHUNK = 128
CHUNKS = V // CHUNK
SPAN = CHUNK * PACK
LIST_COLS = V // 16
HALF = 2 * P
VECTOR_CLEARS = 3 * T // 4
FIRST_PART = 768


def load_scale_rows(nc, plane, rows):
    by_place = rows.rearrange("(q r) c -> r q c", r=PACK)
    for r in range(PACK):
        nc.sync.dma_start(out=plane[r:P:QUADRANT, :].bitcast(I32), in_=by_place[r].bitcast(I32))


def woven(values):
    return values.rearrange("p (v t) -> p v t", t=PACK)


def half_views(rows, u, rounded):
    source = rows.rearrange("p (a b) (m t) -> p m a t b", b=2, t=PACK)[:, :, :, 2 * u : 2 * u + 2, :]
    return rounded.rearrange("p (t m a b) -> p m a t b", t=2, a=2, b=2), source


def tile_picked_trilin_none_p_kernel(
    tc, x_words, x_scales, w1, w2, w3, w4_words, w4_scales, offs, out
):
    nc = tc.nc
    with ExitStack() as ctx:
        keep = ctx.enter_context(tc.tile_pool(name="keep", bufs=1))
        psum = ctx.enter_context(tc.psum_pool(name="psum", bufs=1))

        offsets = keep.tile([P, PIECES * LIST_COLS], U16, name="offsets")
        nc.sync.dma_start(offsets[:], offs)

        store_scales = keep.tile([P, T], U8, name="store_scales")
        nc.vector.memset(store_scales[:, 0:VECTOR_CLEARS].bitcast(I32), 0)
        nc.gpsimd.memset(store_scales[:, VECTOR_CLEARS:T].bitcast(I32), 0)
        load_scale_rows(nc, store_scales, x_scales[0])
        store_words = keep.tile([P, T], U32, name="store_words")
        x_rows = x_words[0].rearrange("p c r -> p (c r)").bitcast(I32)
        for cols in (slice(0, FIRST_PART), slice(FIRST_PART, T)):
            nc.sync.dma_start(out=store_words[:, cols].bitcast(I32), in_=x_rows[:, cols])
        raw = []
        for d, w in enumerate((w1, w2, w3)):
            rows = keep.tile([P, PACK, H], F32, name=f"raw{d}", tag=f"raw{d}")
            nc.sync.dma_start(out=rows[:], in_=w.rearrange("(p j) h -> p j h", j=PACK))
            raw.append(rows)
        w4_codes = keep.tile([P, N], U32, name="w4_codes", align_bytes=64)
        nc.sync.dma_start(
            out=w4_codes[:].bitcast(I32),
            in_=w4_words[0].rearrange("p c r -> p (c r)").bitcast(I32),
        )
        w4_plane = keep.tile([P, N], U8, name="w4_plane", align_bytes=64)
        nc.gpsimd.memset(w4_plane[:].bitcast(I32), 0)
        load_scale_rows(nc, w4_plane, w4_scales[0])

        warm = keep.tile([P, 2, 8], F32, name="warm")
        nc.gpsimd.memset(warm[:, 0, :], 0.0)
        nc.scalar.copy(out=warm[:, 1, :], in_=warm[:, 0, :])

        picked_scales = keep.tile([P, PIECES * V], U8, name="picked_scales", align_bytes=64)
        nc.vector.tensor_copy(picked_scales[:], store_scales[:].indirect(offsets[:]))
        picked_words = []
        for d in range(PIECES):
            words = keep.tile([P, V], U32, name=f"picked_words{d}", align_bytes=64)
            piece = offsets[:, d * LIST_COLS : (d + 1) * LIST_COLS]
            nc.vector.tensor_copy(words[:], store_words[:].indirect(piece))
            picked_words.append(words)

        def quantize(name, rounded):
            width = rounded.shape[1] // PACK
            codes = keep.tile([P, width], U32, name=f"{name}_codes", align_bytes=64)
            plane = keep.tile([P, width], U8, name=f"{name}_plane", align_bytes=64)
            nc.vector.quantize_mx(out=codes[:].bitcast(FP8X4), scales=plane[:], in_=rounded)
            return codes, plane

        def round_half(d, u, copy):
            rounded = keep.tile([P, PACK * HALF], BF16, name=f"rounded{d}_{u}", align_bytes=64)
            target, source = half_views(raw[d][:], u, rounded[:])
            copy(out=target, in_=source)
            return rounded[:]

        def factor(d, halves, c, bank, tile_order):
            acc = psum.tile([P, PACK, CHUNK], F32, name=f"acc{d}_{c}", tag=f"bank{bank}")
            cols = slice(c * CHUNK, (c + 1) * CHUNK)
            scale_cols = slice(d * V + c * CHUNK, d * V + (c + 1) * CHUNK)
            for t in tile_order:
                codes, plane = halves[t // 2]
                w_cols = slice((t % 2) * P, (t % 2 + 1) * P)
                nc.tensor.matmul_mx(
                    out=acc[:, t, :],
                    lhsT=codes[:, w_cols].bitcast(FP8X4),
                    lhsT_scale=plane[:, w_cols],
                    rhs=picked_words[d][:, cols].bitcast(FP8X4),
                    rhs_scale=picked_scales[:, scale_cols],
                    start=True,
                    stop=True,
                )
            return acc[:].rearrange("p t v -> p v t")

        w1_halves = [quantize(f"w1_{u}", round_half(0, u, nc.scalar.copy)) for u in range(2)]
        w2_low = round_half(1, 0, nc.scalar.copy)
        w2_high = round_half(1, 1, nc.vector.tensor_copy)
        w2_high_half = quantize("w2_1", w2_high)
        w2_halves = [quantize("w2_0", w2_low), w2_high_half]

        first_acc, second_acc = [], []
        for c in range(CHUNKS):
            first_acc.append(factor(0, w1_halves, c, c, (0, 1, 2, 3)))
            second_acc.append(factor(1, w2_halves, c, CHUNKS + c, (2, 3, 0, 1)))

        def hold_first(chunks, tag):
            held = keep.tile([P, len(chunks), SPAN], F32, name=f"first{chunks[0]}", tag=tag)
            for place, c in enumerate(chunks):
                nc.scalar.copy(out=woven(held[:, place, :]), in_=first_acc[c])
            return [held[:, place, :] for place in range(len(chunks))]

        def multiply_pair(c, tag):
            both = keep.tile([P, SPAN], F32, name=f"pair{c}", tag=tag, align_bytes=64)
            nc.vector.tensor_tensor(out=woven(both[:]), in0=second_acc[c], in1=woven(first[c]), op=MULT)
            return both

        first = hold_first([0, 1], "first_early")
        w3_rounded = keep.tile([P, 2, PACK * HALF], BF16, name="w3_rounded", tag="w3_rounded", align_bytes=64)
        target, source = half_views(raw[2][:], 0, w3_rounded[:, 0, :])
        nc.scalar.copy(out=target, in_=source)
        nc.gpsimd.tensor_scalar(
            out=w3_rounded[:, 1, :].rearrange("p (t m j) -> p m t j", t=2, j=PACK),
            in0=raw[2][:].rearrange("p j (m t) -> p m t j", t=PACK)[:, :, 2:4, :],
            scalar1=1.0,
            scalar2=0.0,
            op0=MULT,
            op1=ADD,
        )
        first = first + hold_first([2, 3], "raw2")

        pair = [multiply_pair(0, "pair0"), multiply_pair(1, "pair1")]
        w3_codes, w3_plane = quantize("w3", w3_rounded[:].rearrange("p u c -> p (u c)"))
        w3_halves = [(w3_codes[:, u * HALF : (u + 1) * HALF], w3_plane[:, u * HALF : (u + 1) * HALF]) for u in range(2)]
        pair.append(multiply_pair(2, "w3_rounded"))
        second_last = keep.tile([P, SPAN], F32, name="second_last")
        nc.scalar.copy(out=woven(second_last[:]), in_=second_acc[3])
        pair_last = keep.tile([P, SPAN], F32, name="pair3")
        nc.gpsimd.tensor_tensor(out=pair_last[:], in0=second_last[:], in1=first[3], op=MULT)
        pair.append(pair_last)

        def multiply_third(c, z):
            acc = factor(2, w3_halves, c, c, (0, 1, 2, 3))
            nc.vector.tensor_tensor(out=woven(z), in0=acc, in1=woven(pair[c][:]), op=MULT)

        def finish(c, z, banks, copies, queues):
            codes, plane = quantize(f"z{c}", z)
            width = z.shape[1] // PACK
            for block in range(N // P):
                acc = psum.tile([P, width], F32, name=f"out_acc{c}_{block}", tag=f"bank{banks[block]}")
                out_rows = slice(block * P, (block + 1) * P)
                nc.tensor.matmul_mx(
                    out=acc[:],
                    lhsT=w4_codes[:, out_rows].bitcast(FP8X4),
                    lhsT_scale=w4_plane[:, out_rows],
                    rhs=codes[:].bitcast(FP8X4),
                    rhs_scale=plane[:],
                    start=True,
                    stop=True,
                )
                result = keep.tile([P, width], F32, name=f"result{c}_{block}")
                copies[block](out=result[:], in_=acc[:])
                queues[block].dma_start(out=out[out_rows, c * CHUNK : c * CHUNK + width], in_=result[:])

        z01 = keep.tile([P, 2 * SPAN], BF16, name="z01", align_bytes=64)
        z2 = keep.tile([P, SPAN], BF16, name="z2", align_bytes=64)
        z3 = keep.tile([P, SPAN], BF16, name="z3", align_bytes=64)
        on_scalar = (nc.scalar.copy, nc.scalar.copy)
        on_sync = (nc.sync, nc.sync)
        multiply_third(0, z01[:, 0:SPAN])
        multiply_third(1, z01[:, SPAN : 2 * SPAN])
        multiply_third(2, z2[:])
        finish(0, z01[:], (4, 5), on_scalar, on_sync)
        multiply_third(3, z3[:])
        finish(2, z2[:], (6, 7), on_scalar, on_sync)
        finish(3, z3[:], (0, 1), (nc.scalar.copy, nc.vector.tensor_copy), (nc.scalar, nc.sync))
